import numpy as np
import ml_dtypes


def mxq(x, axis, fmt="e4m3"):
    dtype, down = {"e4m3": (ml_dtypes.float8_e4m3fn, 7), "e5m2": (ml_dtypes.float8_e5m2, 14)}[fmt]
    v = np.moveaxis(np.asarray(x, np.float32).astype(ml_dtypes.bfloat16).astype(np.float64), axis, -1)
    blocks = v.reshape(v.shape[:-1] + (-1, 32))
    amax = np.abs(blocks).max(-1, keepdims=True)
    byte = np.maximum(np.where(amax > 0, np.frexp(amax)[1] - 1 + 127, 0) - down, 1)
    scale = np.exp2(byte - 127.0)
    codes = (blocks / scale).astype(np.float32).astype(dtype).astype(np.float64)
    return np.moveaxis((codes * scale).reshape(v.shape), -1, axis)


WIDE = False


def mx_kscale(k):
    if not WIDE:
        return np.ones(k)
    levels = np.array([10, -10, 5, -5, 0])
    if k % 512:
        return np.exp2(np.random.permutation(np.resize(levels, k // 32))).repeat(32)
    a = np.empty((k // 512, 16))
    for p in range(k // 512):
        a[p, :8] = np.random.permutation(np.resize(levels, 8))
        for g in range(8):
            far = levels[np.abs(levels - a[p, g]) >= 10]
            a[p, g + 8] = far[np.random.randint(len(far))]
    return np.exp2(a.ravel()).repeat(32)


def f64(x):
    return np.asarray(x).astype(np.float64)


def striped8(idx):
    return np.asarray(idx).reshape(8, -1, 16).transpose(0, 2, 1).reshape(128, -1).astype(np.uint16)


def unstriped8(offs):
    return offs.reshape(8, 16, -1).transpose(0, 2, 1).reshape(8, -1).astype(np.int64)


def pick8(x, idx, run):
    r = np.arange(len(x))
    return x[r[:, None], idx[r % (8 * run) // run]]


E2M1 = np.array([0.0, 0.5, 1.0, 1.5, 2.0, 3.0, 4.0, 6.0, -0.0, -0.5, -1.0, -1.5, -2.0, -3.0, -4.0, -6.0])


def pack_weight(w, fmt):
    k, n = w.shape
    w = f64(np.asarray(w, np.float32).astype(ml_dtypes.bfloat16)).reshape(k // 32, 32, n)
    amax = np.abs(w).max(1)
    if fmt == "e4m3":
        byte = np.frexp(amax)[1] - 1 + 127 - 7
    else:
        mant, ex = np.frexp(amax / 6.0)
        byte = np.where(mant > 0.5, ex, ex - 1) + 127
    byte = np.clip(np.where(amax > 0, byte, 1), 1, 254)
    scaled = (w * np.exp2(127.0 - byte)[:, None, :]).reshape(k, n).astype(np.float32)
    by_word = np.ascontiguousarray(scaled.reshape(k // 512, 128, 4, n).transpose(0, 1, 3, 2))
    if fmt == "e4m3":
        words = by_word.astype(ml_dtypes.float8_e4m3fn).view(np.uint8)
    else:
        c = by_word.astype(ml_dtypes.float4_e2m1fn).view(np.uint8) & 0xF
        words = (c[..., 0::2] | (c[..., 1::2] << 4)).reshape(k // 512, 128, 2 * n)
    return np.ascontiguousarray(words), np.ascontiguousarray(byte.astype(np.uint8).reshape(k // 512, 16, n))


def unpack_weight(words, scales, fmt):
    g, _, n = scales.shape
    words = np.ascontiguousarray(words).reshape(g, 128, n, -1)
    if fmt == "e4m3":
        vals = words.view(ml_dtypes.float8_e4m3fn).astype(np.float64)
    else:
        nib = np.empty((g, 128, n, 4), np.uint8)
        nib[..., 0::2] = words & 0xF
        nib[..., 1::2] = words >> 4
        vals = E2M1[nib]
    vals = vals * np.repeat(np.exp2(scales.astype(np.float64) - 127.0), 8, axis=1)[..., None]
    return vals.transpose(0, 1, 3, 2).reshape(g * 512, n)


D, T, I, Q = 512, 1024, 512, 128


def setup_inputs():
    n = np.random.standard_normal
    idx = np.stack([np.random.permutation(T)[:I] for _ in range(8)])
    idx2 = np.stack([np.random.permutation(T)[:I] for _ in range(8)])
    idx3 = np.stack([np.random.permutation(T)[:I] for _ in range(8)])
    fd = mx_kscale(D)
    keysp = pack_weight(n((D, T)) / fd[:, None], "e2m1")
    return {
        "query": (n((D, Q)) * 1.2 / np.sqrt(D) * fd[:, None]).astype(np.float32),
        "keys_words": keysp[0],
        "keys_scales": keysp[1],
        "lam": (np.random.uniform(0.2, 0.7, (Q, 1))).astype(np.float32),
        "width": (np.random.uniform(0.3, 0.8, (Q, 1))).astype(np.float32),
        "old": (np.random.uniform(0.0, 2.0, (Q, T))).astype(np.float32),
        "fade": (np.random.uniform(0.3, 0.9, (Q, 1))).astype(np.float32),
        "offs": striped8(idx),
        "offs2": striped8(idx2),
        "offs3": striped8(idx3),
    }


def reference(query, keys_words, keys_scales, lam, width, old, fade, offs, offs2, offs3):
    idx = unstriped8(offs)
    idx2 = unstriped8(offs2)
    idx3 = unstriped8(offs3)
    keysu = unpack_weight(keys_words, keys_scales, "e2m1")
    queryq = mxq(f64(query), 0, "e4m3")
    a = queryq.T @ keysu
    mx3 = np.maximum(np.maximum(pick8(a, idx, 16), pick8(a, idx2, 16)), pick8(a, idx3, 16))
    mn3 = np.minimum(np.minimum(pick8(a, idx, 16), pick8(a, idx2, 16)), pick8(a, idx3, 16))
    s = (pick8(a, idx, 16) + pick8(a, idx2, 16) + pick8(a, idx3, 16)) / 3.0 - (mx3 - mn3) * f64(lam)
    ce = (s - np.mean(s, axis=1, keepdims=True)) / f64(width)
    p = 1.0 / (np.square(ce) + 1.0)
    w = p / np.sum(p, axis=1, keepdims=True)
    ws = w * 512.0
    wf = np.zeros((Q, T))
    wf[np.arange(Q)[:, None], idx[np.arange(Q) % 128 // 16]] = ws
    y = f64(old) * f64(fade) + wf
    return y

@@ -1,0 +1,168 @@
+from contextlib import ExitStack
+
+import concourse.mybir as mybir
+
+D, T, SLOTS, Q = 512, 1024, 512, 128
+FLOPS = 2 * D * Q * T
+
+F32 = mybir.dt.float32
+BF16 = mybir.dt.bfloat16
+I32 = mybir.dt.int32
+U32 = mybir.dt.uint32
+U16 = mybir.dt.uint16
+U8 = mybir.dt.uint8
+FP8X4 = mybir.dt.float8_e4m3fn_x4
+FP4X4 = mybir.dt.float4_e2m1fn_x4
+ALU = mybir.AluOpType
+ACT = mybir.ActivationFunctionType
+
+P = 128
+PACK = 4
+HALF = SLOTS // 2
+LIST_COLS = HALF // 16
+N_MM = 256
+N_OUT = 256
+
+
+def tile_attend_spreadof3_typical_counts_heads_kernel(
+    tc, query, keys_words, keys_scales, lam, width, old, fade, offs, offs2, offs3, out
+):
+    nc = tc.nc
+    with ExitStack() as ctx:
+        keep = ctx.enter_context(tc.tile_pool(name="keep", bufs=1))
+        psum = ctx.enter_context(tc.psum_pool(name="psum", bufs=1))
+
+        list_x = keep.tile([P, SLOTS // 16], U16, name="list_x")
+        list_y = keep.tile([P, SLOTS // 16], U16, name="list_y")
+        list_z = keep.tile([P, SLOTS // 16], U16, name="list_z")
+        q_raw = keep.tile([P, PACK, Q], F32, name="q_raw")
+        k_words = keep.tile([P, 2 * T], U8, name="k_words", align_bytes=64)
+        k_scales = keep.tile([P, T], U8, name="k_scales", align_bytes=64)
+        width_t = keep.tile([P, 1], F32, name="width_t")
+        lam_t = keep.tile([P, 1], F32, name="lam_t")
+        fade_t = keep.tile([P, 1], F32, name="fade_t")
+        old_t = keep.tile([P, T], F32, name="old_t")
+        placed = keep.tile([P, T], F32, name="placed")
+
+        nc.vector.memset(k_scales[:].bitcast(I32), 0)
+        nc.vector.memset(placed[:], 0.0)
+
+        nc.sync.dma_start(out=q_raw[:], in_=query.rearrange("(p j) q -> p j q", j=PACK))
+        nc.sync.dma_start(out=k_words[:].bitcast(I32), in_=keys_words[0].bitcast(I32))
+        for j in range(4):
+            nc.scalar.dma_start(
+                out=k_scales[j:P:32, :].bitcast(I32), in_=keys_scales[0][j:16:4, :].bitcast(I32)
+            )
+        nc.sync.dma_start(out=width_t[:], in_=width)
+        nc.sync.dma_start(list_x[:], offs)
+        nc.sync.dma_start(list_y[:], offs2)
+        nc.sync.dma_start(list_z[:], offs3)
+        nc.sync.dma_start(out=lam_t[:], in_=lam)
+        nc.sync.dma_start(out=fade_t[:], in_=fade)
+        nc.sync.dma_start(out=old_t[:], in_=old)
+
+        w_m12 = keep.tile([P, 1], F32, name="w_m12")
+        w_m1 = keep.tile([P, 1], F32, name="w_m1")
+        w_m2 = keep.tile([P, 1], F32, name="w_m2")
+        nc.scalar.activation(w_m12[:], width_t[:], ACT.Abs_reciprocal_sqrt, scale=3.0 * SLOTS)
+        nc.scalar.activation(w_m1[:], w_m12[:], ACT.Square)
+        nc.scalar.activation(w_m2[:], w_m1[:], ACT.Square)
+        lam_neg = keep.tile([P, 1], F32, name="lam_neg")
+        lam_pos = keep.tile([P, 1], F32, name="lam_pos")
+        nc.gpsimd.tensor_scalar(lam_neg[:], lam_t[:], -3.0, 0.0, ALU.mult, ALU.add)
+        nc.gpsimd.tensor_scalar(lam_pos[:], lam_t[:], 3.0, 0.0, ALU.mult, ALU.add)
+
+        q_bf = keep.tile([P, Q, PACK], BF16, name="q_bf", align_bytes=64)
+        q_codes = keep.tile([P, Q], U32, name="q_codes", align_bytes=64)
+        q_scales = keep.tile([P, Q], U8, name="q_scales", align_bytes=64)
+        nc.vector.tensor_copy(out=q_bf[:], in_=q_raw[:].rearrange("p j q -> p q j"))
+        nc.vector.quantize_mx(
+            out=q_codes[:].bitcast(FP8X4), scales=q_scales[:], in_=q_bf[:].rearrange("p q j -> p (q j)")
+        )
+
+        a = keep.tile([P, T], F32, name="a")
+        for b in range(T // N_MM):
+            cols = slice(b * N_MM, (b + 1) * N_MM)
+            bank = psum.tile([P, N_MM], F32, name="bank%d" % b)
+            nc.tensor.matmul_mx(
+                out=bank[:],
+                lhsT=q_codes[:].bitcast(FP8X4),
+                lhsT_scale=q_scales[:],
+                rhs=k_words[:, 2 * b * N_MM : 2 * (b + 1) * N_MM].bitcast(FP4X4),
+                rhs_scale=k_scales[:, cols],
+                start=True,
+                stop=True,
+            )
+            if b % 2 == 0:
+                nc.vector.tensor_copy(out=a[:, cols], in_=bank[:])
+            else:
+                nc.scalar.copy(out=a[:, cols], in_=bank[:])
+
+        def looked_up(lst, half):
+            return a[:].indirect(lst[:, half * LIST_COLS : (half + 1) * LIST_COLS])
+
+        def half_tile(name):
+            return keep.tile([P, HALF], F32, name=name)
+
+        x_a, y_a, z_a, x_b, y_b, z_b = [half_tile(n) for n in ("x_a", "y_a", "z_a", "x_b", "y_b", "z_b")]
+        nc.vector.tensor_copy(out=y_a[:], in_=looked_up(list_y, 0))
+        nc.scalar.activation(x_a[:], looked_up(list_x, 0), ACT.Copy)
+        nc.scalar.activation(z_a[:], looked_up(list_z, 0), ACT.Copy)
+        nc.scalar.activation(x_b[:], looked_up(list_x, 1), ACT.Copy)
+        nc.scalar.activation(y_b[:], looked_up(list_y, 1), ACT.Copy)
+        nc.scalar.activation(z_b[:], looked_up(list_z, 1), ACT.Copy)
+
+        def column(name):
+            return keep.tile([P, 1], F32, name=name)
+
+        s3 = keep.tile([P, SLOTS], F32, name="s3")
+
+        def scores(half, x, y, z, total_sum, hi_sum, lo_sum, s_sum):
+            u, v, pair, total, hi, lo, spread = [
+                half_tile("%s%d" % (n, half)) for n in ("u", "v", "pair", "total", "hi", "lo", "spread")
+            ]
+            nc.vector.tensor_tensor(u[:], x[:], y[:], ALU.max)
+            nc.vector.tensor_tensor(v[:], x[:], y[:], ALU.min)
+            nc.vector.tensor_tensor(pair[:], x[:], y[:], ALU.add)
+            nc.vector.scalar_tensor_tensor(hi[:], u[:], 1.0, z[:], ALU.mult, ALU.max, accum_out=hi_sum)
+            nc.vector.scalar_tensor_tensor(total[:], pair[:], 1.0, z[:], ALU.mult, ALU.add, accum_out=total_sum)
+            nc.vector.scalar_tensor_tensor(lo[:], v[:], 1.0, z[:], ALU.mult, ALU.min, accum_out=lo_sum)
+            nc.vector.tensor_tensor(spread[:], hi[:], lo[:], ALU.subtract)
+            nc.vector.scalar_tensor_tensor(
+                s3[:, half * HALF : (half + 1) * HALF], spread[:], lam_neg[:], total[:], ALU.mult, ALU.add,
+                accum_out=s_sum,
+            )
+
+        s_sum_a, total_sum_b, hi_sum_b, lo_sum_b = [column(n) for n in ("s_sum_a", "total_sum_b", "hi_sum_b", "lo_sum_b")]
+        scores(0, x_a, y_a, z_a, None, None, None, s_sum_a[:])
+        scores(1, x_b, y_b, z_b, total_sum_b[:], hi_sum_b[:], lo_sum_b[:], None)
+
+        sum0, sum1, sum2 = column("sum0"), column("sum1"), column("sum2")
+        nc.scalar.activation(sum0[:], hi_sum_b[:], ACT.Identity, scale=lam_neg[:], bias=s_sum_a[:])
+        nc.scalar.activation(sum1[:], total_sum_b[:], ACT.Identity, bias=sum0[:])
+        nc.scalar.activation(sum2[:], lo_sum_b[:], ACT.Identity, scale=lam_pos[:], bias=sum1[:])
+
+        dev2 = keep.tile([P, SLOTS], F32, name="dev2", tag="dev2_then_faded")
+        root = keep.tile([P, SLOTS], F32, name="root")
+        for half in range(2):
+            slots = slice(half * HALF, (half + 1) * HALF)
+            nc.scalar.activation(dev2[:, slots], s3[:, slots], ACT.Square, scale=-float(SLOTS), bias=sum2[:])
+            nc.scalar.activation(root[:, slots], dev2[:, slots], ACT.Abs_reciprocal_sqrt, scale=w_m2[:], bias=1.0)
+        part_mean, norm = column("part_mean"), column("norm")
+        parts = keep.tile([P, SLOTS], F32, name="parts")
+        nc.scalar.activation(parts[:], root[:], ACT.Square, scale=SLOTS**-0.5, accum_out=part_mean[:])
+        faded = keep.tile([P, T], F32, name="faded", tag="dev2_then_faded")
+        nc.scalar.activation(faded[:], old_t[:], ACT.Copy, scale=fade_t[:])
+
+        for half in range(2):
+            slots = slice(half * HALF, (half + 1) * HALF)
+            window = placed[:].indirect(list_x[:, half * LIST_COLS : (half + 1) * LIST_COLS])
+            nc.vector.tensor_tensor(window, root[:, slots], root[:, slots], ALU.mult)
+        nc.vector.reciprocal(norm[:], part_mean[:])
+
+        for c in range(T // N_OUT):
+            cols = slice(c * N_OUT, (c + 1) * N_OUT)
+            result = keep.tile([P, N_OUT], F32, name="result%d" % c)
+            nc.vector.scalar_tensor_tensor(result[:], placed[:, cols], norm[:], faded[:, cols], ALU.mult, ALU.add)
+            queue = nc.sync if c % 2 == 0 else nc.scalar
+            queue.dma_start(out=out[:, cols], in_=result[:])

@@ -20,7 +20,8 @@ P = 128
 PACK = 4
 HALF = SLOTS // 2
 LIST_COLS = HALF // 16
-N_MM = 256
+MM_WIDTHS = (256, 256, 256, 128, 128)
+FIRST = 192
 N_OUT = 256
 
 
@@ -53,10 +54,10 @@ def tile_attend_spreadof3_typical_counts_heads_kernel(
             nc.scalar.dma_start(
                 out=k_scales[j:P:32, :].bitcast(I32), in_=keys_scales[0][j:16:4, :].bitcast(I32)
             )
-        nc.sync.dma_start(out=width_t[:], in_=width)
+        nc.gpsimd.dma_start(out=width_t[:], in_=width)
         nc.sync.dma_start(list_x[:], offs)
-        nc.sync.dma_start(list_y[:], offs2)
         nc.sync.dma_start(list_z[:], offs3)
+        nc.sync.dma_start(list_y[:], offs2)
         nc.sync.dma_start(out=lam_t[:], in_=lam)
         nc.sync.dma_start(out=fade_t[:], in_=fade)
         nc.sync.dma_start(out=old_t[:], in_=old)
@@ -65,12 +66,12 @@ def tile_attend_spreadof3_typical_counts_heads_kernel(
         w_m1 = keep.tile([P, 1], F32, name="w_m1")
         w_m2 = keep.tile([P, 1], F32, name="w_m2")
         nc.scalar.activation(w_m12[:], width_t[:], ACT.Abs_reciprocal_sqrt, scale=3.0 * SLOTS)
-        nc.scalar.activation(w_m1[:], w_m12[:], ACT.Square)
-        nc.scalar.activation(w_m2[:], w_m1[:], ACT.Square)
+        nc.gpsimd.tensor_tensor(w_m1[:], w_m12[:], w_m12[:], ALU.mult)
+        nc.gpsimd.tensor_tensor(w_m2[:], w_m1[:], w_m1[:], ALU.mult)
         lam_neg = keep.tile([P, 1], F32, name="lam_neg")
         lam_pos = keep.tile([P, 1], F32, name="lam_pos")
-        nc.gpsimd.tensor_scalar(lam_neg[:], lam_t[:], -3.0, 0.0, ALU.mult, ALU.add)
         nc.gpsimd.tensor_scalar(lam_pos[:], lam_t[:], 3.0, 0.0, ALU.mult, ALU.add)
+        nc.gpsimd.tensor_scalar(lam_neg[:], lam_t[:], -3.0, 0.0, ALU.mult, ALU.add)
 
         q_bf = keep.tile([P, Q, PACK], BF16, name="q_bf", align_bytes=64)
         q_codes = keep.tile([P, Q], U32, name="q_codes", align_bytes=64)
@@ -81,14 +82,15 @@ def tile_attend_spreadof3_typical_counts_heads_kernel(
         )
 
         a = keep.tile([P, T], F32, name="a")
-        for b in range(T // N_MM):
-            cols = slice(b * N_MM, (b + 1) * N_MM)
-            bank = psum.tile([P, N_MM], F32, name="bank%d" % b)
+        for b, n in enumerate(MM_WIDTHS):
+            c0 = sum(MM_WIDTHS[:b])
+            cols = slice(c0, c0 + n)
+            bank = psum.tile([P, n], F32, name="bank%d" % b)
             nc.tensor.matmul_mx(
                 out=bank[:],
                 lhsT=q_codes[:].bitcast(FP8X4),
                 lhsT_scale=q_scales[:],
-                rhs=k_words[:, 2 * b * N_MM : 2 * (b + 1) * N_MM].bitcast(FP4X4),
+                rhs=k_words[:, 2 * c0 : 2 * (c0 + n)].bitcast(FP4X4),
                 rhs_scale=k_scales[:, cols],
                 start=True,
                 stop=True,
@@ -109,54 +111,56 @@ def tile_attend_spreadof3_typical_counts_heads_kernel(
         nc.scalar.activation(x_a[:], looked_up(list_x, 0), ACT.Copy)
         nc.scalar.activation(z_a[:], looked_up(list_z, 0), ACT.Copy)
         nc.scalar.activation(x_b[:], looked_up(list_x, 1), ACT.Copy)
-        nc.scalar.activation(y_b[:], looked_up(list_y, 1), ACT.Copy)
         nc.scalar.activation(z_b[:], looked_up(list_z, 1), ACT.Copy)
+        nc.scalar.activation(y_b[:], looked_up(list_y, 1), ACT.Copy)
 
         def column(name):
             return keep.tile([P, 1], F32, name=name)
 
         s3 = keep.tile([P, SLOTS], F32, name="s3")
 
-        def scores(half, x, y, z, total_sum, hi_sum, lo_sum, s_sum):
-            u, v, pair, total, hi, lo, spread = [
-                half_tile("%s%d" % (n, half)) for n in ("u", "v", "pair", "total", "hi", "lo", "spread")
+        def scores(half, x, y, z, hi_sum, total_sum, lo_sum, s_sum):
+            tags = ("u", "v", "hi", "lo") if half == 0 else ("hi", "lo", "u", "v")
+            u, v, hi, lo = [
+                keep.tile([P, HALF], F32, name="%s%d" % (n, half), tag=t) for n, t in zip(("u", "v", "hi", "lo"), tags)
             ]
+            pair, total = half_tile("pair"), half_tile("total")
+            less_hi = half_tile("less_hi%d" % half)
+            nc.vector.tensor_tensor(pair[:], x[:], y[:], ALU.add)
             nc.vector.tensor_tensor(u[:], x[:], y[:], ALU.max)
             nc.vector.tensor_tensor(v[:], x[:], y[:], ALU.min)
-            nc.vector.tensor_tensor(pair[:], x[:], y[:], ALU.add)
-            nc.vector.scalar_tensor_tensor(hi[:], u[:], 1.0, z[:], ALU.mult, ALU.max, accum_out=hi_sum)
             nc.vector.scalar_tensor_tensor(total[:], pair[:], 1.0, z[:], ALU.mult, ALU.add, accum_out=total_sum)
+            nc.vector.scalar_tensor_tensor(hi[:], u[:], 1.0, z[:], ALU.mult, ALU.max, accum_out=hi_sum)
             nc.vector.scalar_tensor_tensor(lo[:], v[:], 1.0, z[:], ALU.mult, ALU.min, accum_out=lo_sum)
-            nc.vector.tensor_tensor(spread[:], hi[:], lo[:], ALU.subtract)
+            nc.vector.scalar_tensor_tensor(less_hi[:], hi[:], lam_neg[:], total[:], ALU.mult, ALU.add)
             nc.vector.scalar_tensor_tensor(
-                s3[:, half * HALF : (half + 1) * HALF], spread[:], lam_neg[:], total[:], ALU.mult, ALU.add,
+                s3[:, half * HALF : (half + 1) * HALF], lo[:], lam_pos[:], less_hi[:], ALU.mult, ALU.add,
                 accum_out=s_sum,
             )
 
         s_sum_a, total_sum_b, hi_sum_b, lo_sum_b = [column(n) for n in ("s_sum_a", "total_sum_b", "hi_sum_b", "lo_sum_b")]
         scores(0, x_a, y_a, z_a, None, None, None, s_sum_a[:])
-        scores(1, x_b, y_b, z_b, total_sum_b[:], hi_sum_b[:], lo_sum_b[:], None)
+        scores(1, x_b, z_b, y_b, hi_sum_b[:], total_sum_b[:], lo_sum_b[:], None)
 
         sum0, sum1, sum2 = column("sum0"), column("sum1"), column("sum2")
-        nc.scalar.activation(sum0[:], hi_sum_b[:], ACT.Identity, scale=lam_neg[:], bias=s_sum_a[:])
-        nc.scalar.activation(sum1[:], total_sum_b[:], ACT.Identity, bias=sum0[:])
+        nc.scalar.activation(sum0[:], total_sum_b[:], ACT.Identity, bias=s_sum_a[:])
+        nc.scalar.activation(sum1[:], hi_sum_b[:], ACT.Identity, scale=lam_neg[:], bias=sum0[:])
         nc.scalar.activation(sum2[:], lo_sum_b[:], ACT.Identity, scale=lam_pos[:], bias=sum1[:])
 
-        dev2 = keep.tile([P, SLOTS], F32, name="dev2", tag="dev2_then_faded")
         root = keep.tile([P, SLOTS], F32, name="root")
-        for half in range(2):
-            slots = slice(half * HALF, (half + 1) * HALF)
-            nc.scalar.activation(dev2[:, slots], s3[:, slots], ACT.Square, scale=-float(SLOTS), bias=sum2[:])
-            nc.scalar.activation(root[:, slots], dev2[:, slots], ACT.Abs_reciprocal_sqrt, scale=w_m2[:], bias=1.0)
+        pieces = (slice(0, FIRST), slice(FIRST, SLOTS))
+        for slots in pieces:
+            dev2 = keep.tile([P, slots.stop - slots.start], F32, name="dev2", tag="dev2_then_faded")
+            nc.scalar.activation(dev2[:], s3[:, slots], ACT.Square, scale=-float(SLOTS), bias=sum2[:])
+            nc.scalar.activation(root[:, slots], dev2[:], ACT.Abs_reciprocal_sqrt, scale=w_m2[:], bias=1.0)
         part_mean, norm = column("part_mean"), column("norm")
         parts = keep.tile([P, SLOTS], F32, name="parts")
         nc.scalar.activation(parts[:], root[:], ACT.Square, scale=SLOTS**-0.5, accum_out=part_mean[:])
         faded = keep.tile([P, T], F32, name="faded", tag="dev2_then_faded")
         nc.scalar.activation(faded[:], old_t[:], ACT.Copy, scale=fade_t[:])
 
-        for half in range(2):
-            slots = slice(half * HALF, (half + 1) * HALF)
-            window = placed[:].indirect(list_x[:, half * LIST_COLS : (half + 1) * LIST_COLS])
+        for slots in pieces:
+            window = placed[:].indirect(list_x[:, slots.start // 16 : slots.stop // 16])
             nc.vector.tensor_tensor(window, root[:, slots], root[:, slots], ALU.mult)
         nc.vector.reciprocal(norm[:], part_mean[:])
 

from contextlib import ExitStack

import concourse.mybir as mybir

D, T, SLOTS, Q = 512, 1024, 512, 128
FLOPS = 2 * D * Q * T

F32 = mybir.dt.float32
BF16 = mybir.dt.bfloat16
I32 = mybir.dt.int32
U32 = mybir.dt.uint32
U16 = mybir.dt.uint16
U8 = mybir.dt.uint8
FP8X4 = mybir.dt.float8_e4m3fn_x4
FP4X4 = mybir.dt.float4_e2m1fn_x4
ALU = mybir.AluOpType
ACT = mybir.ActivationFunctionType

P = 128
PACK = 4
HALF = SLOTS // 2
LIST_COLS = HALF // 16
MM_WIDTHS = (256, 256, 256, 128, 128)
FIRST = 192
N_OUT = 256


def tile_attend_spreadof3_typical_counts_heads_kernel(
    tc, query, keys_words, keys_scales, lam, width, old, fade, offs, offs2, offs3, out
):
    nc = tc.nc
    with ExitStack() as ctx:
        keep = ctx.enter_context(tc.tile_pool(name="keep", bufs=1))
        psum = ctx.enter_context(tc.psum_pool(name="psum", bufs=1))

        list_x = keep.tile([P, SLOTS // 16], U16, name="list_x")
        list_y = keep.tile([P, SLOTS // 16], U16, name="list_y")
        list_z = keep.tile([P, SLOTS // 16], U16, name="list_z")
        q_raw = keep.tile([P, PACK, Q], F32, name="q_raw")
        k_words = keep.tile([P, 2 * T], U8, name="k_words", align_bytes=64)
        k_scales = keep.tile([P, T], U8, name="k_scales", align_bytes=64)
        width_t = keep.tile([P, 1], F32, name="width_t")
        lam_t = keep.tile([P, 1], F32, name="lam_t")
        fade_t = keep.tile([P, 1], F32, name="fade_t")
        old_t = keep.tile([P, T], F32, name="old_t")
        placed = keep.tile([P, T], F32, name="placed")

        nc.vector.memset(k_scales[:].bitcast(I32), 0)
        nc.vector.memset(placed[:], 0.0)

        nc.sync.dma_start(out=q_raw[:], in_=query.rearrange("(p j) q -> p j q", j=PACK))
        nc.sync.dma_start(out=k_words[:].bitcast(I32), in_=keys_words[0].bitcast(I32))
        for j in range(4):
            nc.scalar.dma_start(
                out=k_scales[j:P:32, :].bitcast(I32), in_=keys_scales[0][j:16:4, :].bitcast(I32)
            )
        nc.gpsimd.dma_start(out=width_t[:], in_=width)
        nc.sync.dma_start(list_x[:], offs)
        nc.sync.dma_start(list_z[:], offs3)
        nc.sync.dma_start(list_y[:], offs2)
        nc.sync.dma_start(out=lam_t[:], in_=lam)
        nc.sync.dma_start(out=fade_t[:], in_=fade)
        nc.sync.dma_start(out=old_t[:], in_=old)

        w_m12 = keep.tile([P, 1], F32, name="w_m12")
        w_m1 = keep.tile([P, 1], F32, name="w_m1")
        w_m2 = keep.tile([P, 1], F32, name="w_m2")
        nc.scalar.activation(w_m12[:], width_t[:], ACT.Abs_reciprocal_sqrt, scale=3.0 * SLOTS)
        nc.gpsimd.tensor_tensor(w_m1[:], w_m12[:], w_m12[:], ALU.mult)
        nc.gpsimd.tensor_tensor(w_m2[:], w_m1[:], w_m1[:], ALU.mult)
        lam_neg = keep.tile([P, 1], F32, name="lam_neg")
        lam_pos = keep.tile([P, 1], F32, name="lam_pos")
        nc.gpsimd.tensor_scalar(lam_pos[:], lam_t[:], 3.0, 0.0, ALU.mult, ALU.add)
        nc.gpsimd.tensor_scalar(lam_neg[:], lam_t[:], -3.0, 0.0, ALU.mult, ALU.add)

        q_bf = keep.tile([P, Q, PACK], BF16, name="q_bf", align_bytes=64)
        q_codes = keep.tile([P, Q], U32, name="q_codes", align_bytes=64)
        q_scales = keep.tile([P, Q], U8, name="q_scales", align_bytes=64)
        nc.vector.tensor_copy(out=q_bf[:], in_=q_raw[:].rearrange("p j q -> p q j"))
        nc.vector.quantize_mx(
            out=q_codes[:].bitcast(FP8X4), scales=q_scales[:], in_=q_bf[:].rearrange("p q j -> p (q j)")
        )

        a = keep.tile([P, T], F32, name="a")
        for b, n in enumerate(MM_WIDTHS):
            c0 = sum(MM_WIDTHS[:b])
            cols = slice(c0, c0 + n)
            bank = psum.tile([P, n], F32, name="bank%d" % b)
            nc.tensor.matmul_mx(
                out=bank[:],
                lhsT=q_codes[:].bitcast(FP8X4),
                lhsT_scale=q_scales[:],
                rhs=k_words[:, 2 * c0 : 2 * (c0 + n)].bitcast(FP4X4),
                rhs_scale=k_scales[:, cols],
                start=True,
                stop=True,
            )
            if b % 2 == 0:
                nc.vector.tensor_copy(out=a[:, cols], in_=bank[:])
            else:
                nc.scalar.copy(out=a[:, cols], in_=bank[:])

        def looked_up(lst, half):
            return a[:].indirect(lst[:, half * LIST_COLS : (half + 1) * LIST_COLS])

        def half_tile(name):
            return keep.tile([P, HALF], F32, name=name)

        x_a, y_a, z_a, x_b, y_b, z_b = [half_tile(n) for n in ("x_a", "y_a", "z_a", "x_b", "y_b", "z_b")]
        nc.vector.tensor_copy(out=y_a[:], in_=looked_up(list_y, 0))
        nc.scalar.activation(x_a[:], looked_up(list_x, 0), ACT.Copy)
        nc.scalar.activation(z_a[:], looked_up(list_z, 0), ACT.Copy)
        nc.scalar.activation(x_b[:], looked_up(list_x, 1), ACT.Copy)
        nc.scalar.activation(z_b[:], looked_up(list_z, 1), ACT.Copy)
        nc.scalar.activation(y_b[:], looked_up(list_y, 1), ACT.Copy)

        def column(name):
            return keep.tile([P, 1], F32, name=name)

        s3 = keep.tile([P, SLOTS], F32, name="s3")

        def scores(half, x, y, z, hi_sum, total_sum, lo_sum, s_sum):
            tags = ("u", "v", "hi", "lo") if half == 0 else ("hi", "lo", "u", "v")
            u, v, hi, lo = [
                keep.tile([P, HALF], F32, name="%s%d" % (n, half), tag=t) for n, t in zip(("u", "v", "hi", "lo"), tags)
            ]
            pair, total = half_tile("pair"), half_tile("total")
            less_hi = half_tile("less_hi%d" % half)
            nc.vector.tensor_tensor(pair[:], x[:], y[:], ALU.add)
            nc.vector.tensor_tensor(u[:], x[:], y[:], ALU.max)
            nc.vector.tensor_tensor(v[:], x[:], y[:], ALU.min)
            nc.vector.scalar_tensor_tensor(total[:], pair[:], 1.0, z[:], ALU.mult, ALU.add, accum_out=total_sum)
            nc.vector.scalar_tensor_tensor(hi[:], u[:], 1.0, z[:], ALU.mult, ALU.max, accum_out=hi_sum)
            nc.vector.scalar_tensor_tensor(lo[:], v[:], 1.0, z[:], ALU.mult, ALU.min, accum_out=lo_sum)
            nc.vector.scalar_tensor_tensor(less_hi[:], hi[:], lam_neg[:], total[:], ALU.mult, ALU.add)
            nc.vector.scalar_tensor_tensor(
                s3[:, half * HALF : (half + 1) * HALF], lo[:], lam_pos[:], less_hi[:], ALU.mult, ALU.add,
                accum_out=s_sum,
            )

        s_sum_a, total_sum_b, hi_sum_b, lo_sum_b = [column(n) for n in ("s_sum_a", "total_sum_b", "hi_sum_b", "lo_sum_b")]
        scores(0, x_a, y_a, z_a, None, None, None, s_sum_a[:])
        scores(1, x_b, z_b, y_b, hi_sum_b[:], total_sum_b[:], lo_sum_b[:], None)

        sum0, sum1, sum2 = column("sum0"), column("sum1"), column("sum2")
        nc.scalar.activation(sum0[:], total_sum_b[:], ACT.Identity, bias=s_sum_a[:])
        nc.scalar.activation(sum1[:], hi_sum_b[:], ACT.Identity, scale=lam_neg[:], bias=sum0[:])
        nc.scalar.activation(sum2[:], lo_sum_b[:], ACT.Identity, scale=lam_pos[:], bias=sum1[:])

        root = keep.tile([P, SLOTS], F32, name="root")
        pieces = (slice(0, FIRST), slice(FIRST, SLOTS))
        for slots in pieces:
            dev2 = keep.tile([P, slots.stop - slots.start], F32, name="dev2", tag="dev2_then_faded")
            nc.scalar.activation(dev2[:], s3[:, slots], ACT.Square, scale=-float(SLOTS), bias=sum2[:])
            nc.scalar.activation(root[:, slots], dev2[:], ACT.Abs_reciprocal_sqrt, scale=w_m2[:], bias=1.0)
        part_mean, norm = column("part_mean"), column("norm")
        parts = keep.tile([P, SLOTS], F32, name="parts")
        nc.scalar.activation(parts[:], root[:], ACT.Square, scale=SLOTS**-0.5, accum_out=part_mean[:])
        faded = keep.tile([P, T], F32, name="faded", tag="dev2_then_faded")
        nc.scalar.activation(faded[:], old_t[:], ACT.Copy, scale=fade_t[:])

        for slots in pieces:
            window = placed[:].indirect(list_x[:, slots.start // 16 : slots.stop // 16])
            nc.vector.tensor_tensor(window, root[:, slots], root[:, slots], ALU.mult)
        nc.vector.reciprocal(norm[:], part_mean[:])

        for c in range(T // N_OUT):
            cols = slice(c * N_OUT, (c + 1) * N_OUT)
            result = keep.tile([P, N_OUT], F32, name="result%d" % c)
            nc.vector.scalar_tensor_tensor(result[:], placed[:, cols], norm[:], faded[:, cols], ALU.mult, ALU.add)
            queue = nc.sync if c % 2 == 0 else nc.scalar
            queue.dma_start(out=out[:, cols], in_=result[:])
